import numpy as np
import ml_dtypes


def mxq(x, axis, fmt="e4m3"):
    dtype, down = {"e4m3": (ml_dtypes.float8_e4m3fn, 7), "e5m2": (ml_dtypes.float8_e5m2, 14)}[fmt]
    v = np.moveaxis(np.asarray(x, np.float32).astype(ml_dtypes.bfloat16).astype(np.float64), axis, -1)
    blocks = v.reshape(v.shape[:-1] + (-1, 32))
    amax = np.abs(blocks).max(-1, keepdims=True)
    byte = np.maximum(np.where(amax > 0, np.frexp(amax)[1] - 1 + 127, 0) - down, 1)
    scale = np.exp2(byte - 127.0)
    codes = (blocks / scale).astype(np.float32).astype(dtype).astype(np.float64)
    return np.moveaxis((codes * scale).reshape(v.shape), -1, axis)


WIDE = False


def mx_kscale(k):
    if not WIDE:
        return np.ones(k)
    levels = np.array([10, -10, 5, -5, 0])
    if k % 512:
        return np.exp2(np.random.permutation(np.resize(levels, k // 32))).repeat(32)
    a = np.empty((k // 512, 16))
    for p in range(k // 512):
        a[p, :8] = np.random.permutation(np.resize(levels, 8))
        for g in range(8):
            far = levels[np.abs(levels - a[p, g]) >= 10]
            a[p, g + 8] = far[np.random.randint(len(far))]
    return np.exp2(a.ravel()).repeat(32)


def f64(x):
    return np.asarray(x).astype(np.float64)


def striped(idx):
    return np.tile(np.asarray(idx).reshape(-1, 16).T, (8, 1)).astype(np.uint16)


def unstriped(offs):
    return offs[:16].T.reshape(-1).astype(np.int64)


E2M1 = np.array([0.0, 0.5, 1.0, 1.5, 2.0, 3.0, 4.0, 6.0, -0.0, -0.5, -1.0, -1.5, -2.0, -3.0, -4.0, -6.0])


def pack_weight(w, fmt):
    k, n = w.shape
    w = f64(np.asarray(w, np.float32).astype(ml_dtypes.bfloat16)).reshape(k // 32, 32, n)
    amax = np.abs(w).max(1)
    if fmt == "e4m3":
        byte = np.frexp(amax)[1] - 1 + 127 - 7
    else:
        mant, ex = np.frexp(amax / 6.0)
        byte = np.where(mant > 0.5, ex, ex - 1) + 127
    byte = np.clip(np.where(amax > 0, byte, 1), 1, 254)
    scaled = (w * np.exp2(127.0 - byte)[:, None, :]).reshape(k, n).astype(np.float32)
    by_word = np.ascontiguousarray(scaled.reshape(k // 512, 128, 4, n).transpose(0, 1, 3, 2))
    if fmt == "e4m3":
        words = by_word.astype(ml_dtypes.float8_e4m3fn).view(np.uint8)
    else:
        c = by_word.astype(ml_dtypes.float4_e2m1fn).view(np.uint8) & 0xF
        words = (c[..., 0::2] | (c[..., 1::2] << 4)).reshape(k // 512, 128, 2 * n)
    return np.ascontiguousarray(words), np.ascontiguousarray(byte.astype(np.uint8).reshape(k // 512, 16, n))


def unpack_weight(words, scales, fmt):
    g, _, n = scales.shape
    words = np.ascontiguousarray(words).reshape(g, 128, n, -1)
    if fmt == "e4m3":
        vals = words.view(ml_dtypes.float8_e4m3fn).astype(np.float64)
    else:
        nib = np.empty((g, 128, n, 4), np.uint8)
        nib[..., 0::2] = words & 0xF
        nib[..., 1::2] = words >> 4
        vals = E2M1[nib]
    vals = vals * np.repeat(np.exp2(scales.astype(np.float64) - 127.0), 8, axis=1)[..., None]
    return vals.transpose(0, 1, 3, 2).reshape(g * 512, n)


def sigmoid(v):
    return 1.0 / (1.0 + np.exp(-v))


K, R, F, T, J, M, N = 512, 128, 512, 2048, 512, 512, 64


def setup_inputs():
    n = np.random.standard_normal
    idx = np.random.permutation(T)[:J]
    idx2 = np.random.permutation(J)[:M]
    idx3 = np.random.permutation(M)[:N]
    fk = mx_kscale(K)
    ff = mx_kscale(F)
    tabp = pack_weight(n((K, T)) / fk[:, None], "e4m3")
    dtabp = pack_weight(n((K, T)) / fk[:, None], "e4m3")
    return {
        "tab_words": tabp[0],
        "tab_scales": tabp[1],
        "w1": (n((K, R)) * 1 / np.sqrt(K) * fk[:, None]).astype(np.float32),
        "gain": (np.random.uniform(0.5, 1.5, (R, 1))).astype(np.float32),
        "pb": (np.random.uniform(-0.5, 0.5, (1, M))).astype(np.float32),
        "mix": (np.random.uniform(0.7, 2.0, (R, 1))).astype(np.float32),
        "wo": (n((F, R)) * 1 / np.sqrt(F) * ff[:, None]).astype(np.float32),
        "dy": (n((F, N)) / ff[:, None]).astype(np.float32),
        "dtab_words": dtabp[0],
        "dtab_scales": dtabp[1],
        "og": (np.random.uniform(0.7, 2.0, (R, 1))).astype(np.float32),
        "base": (0.3 * n((R, J))).astype(np.float32),
        "offs": striped(idx),
        "offs2": striped(idx2),
        "offs3": striped(idx3),
    }


def reference(tab_words, tab_scales, w1, gain, pb, mix, wo, dy, dtab_words, dtab_scales, og, base, offs, offs2, offs3):
    idx = unstriped(offs)
    idx2 = unstriped(offs2)
    idx3 = unstriped(offs3)
    tabu = unpack_weight(tab_words, tab_scales, "e4m3")
    dtabu = unpack_weight(dtab_words, dtab_scales, "e4m3")
    w1q = mxq(f64(w1), 0, "e4m3")
    tabidxg = tabu[:, idx]
    a = w1q.T @ tabidxg
    dtabidxg = dtabu[:, idx]
    ta = w1q.T @ dtabidxg
    h1 = np.tanh(a)
    h2 = h1 * f64(gain)
    s = h2[:, idx2] + f64(pb)
    v1 = s[:, idx3] * f64(mix)
    woq = mxq(f64(wo), 0, "e4m3")
    dyq = mxq(f64(dy), 0, "e4m3")
    c0 = woq.T @ dyq
    dv1 = c0 * sigmoid(v1) * (1.0 + v1 * (1.0 - sigmoid(v1)))
    e1 = dv1 * f64(mix)
    s1 = np.zeros((R, M))
    s1[:, idx3] = e1
    s2 = np.zeros((R, J))
    s2[:, idx2] = s1
    dh1 = s2 * f64(gain)
    xh1 = ta * (1.0 - np.square(h1))
    xh2 = xh1 * f64(gain)
    xs = xh2[:, idx2]
    xv1 = xs[:, idx3] * f64(mix)
    xdv1 = (xv1 * sigmoid(v1) * (1.0 - sigmoid(v1)) * (1.0 + v1 * (1.0 - sigmoid(v1))) + (xv1 * (1.0 - sigmoid(v1)) + xv1 * sigmoid(v1) * (1.0 - sigmoid(v1)) * (-1.0) * v1) * sigmoid(v1)) * c0
    xe1 = xdv1 * f64(mix)
    xs1 = np.zeros((R, M))
    xs1[:, idx3] = xe1
    xs2 = np.zeros((R, J))
    xs2[:, idx2] = xs1
    xdh1 = xs2 * f64(gain)
    xda = xdh1 * (1.0 - np.square(h1)) + xh1 * h1 * 2.0 * (-1.0) * dh1
    y = xda * f64(og) + f64(base)
    return y

@@ -1,0 +1,200 @@
+from contextlib import ExitStack
+
+import concourse.mybir as mybir
+from concourse.masks import make_identity
+
+K, R, F, T, J, M, N = 512, 128, 512, 2048, 512, 512, 64
+FLOPS = 2 * (2 * K * R * J + F * R * N)
+
+F32 = mybir.dt.float32
+BF16 = mybir.dt.bfloat16
+I32 = mybir.dt.int32
+U32 = mybir.dt.uint32
+U16 = mybir.dt.uint16
+U8 = mybir.dt.uint8
+FP8X4 = mybir.dt.float8_e4m3fn_x4
+ACT = mybir.ActivationFunctionType
+MULT = mybir.AluOpType.mult
+ADD = mybir.AluOpType.add
+SUB = mybir.AluOpType.subtract
+
+P = 128
+PACK = 4
+WIDE = 704
+
+
+def tile_attend_hvtwohops_kernel(tc, tab_words, tab_scales, w1, gain, pb, mix, wo, dy, dtab_words, dtab_scales,
+                                  og, base, offs, offs2, offs3, out):
+    nc = tc.nc
+    with ExitStack() as ctx:
+        lists = ctx.enter_context(tc.tile_pool(name="lists", bufs=1))
+        sb = ctx.enter_context(tc.tile_pool(name="sb", bufs=1))
+        psum = ctx.enter_context(tc.psum_pool(name="psum", bufs=1))
+
+        idx = lists.tile([P, J // 16], U16, name="idx")
+        idx2 = lists.tile([P, M // 16], U16, name="idx2")
+        idx3 = lists.tile([P, N // 16], U16, name="idx3")
+
+        tab_s = sb.tile([P, T], U8, name="tab_s", tag="tab_s", align_bytes=64)
+        dtab_s = sb.tile([P, T], U8, name="dtab_s", tag="dtab_s", align_bytes=64)
+        h2 = sb.tile([P, WIDE], F32, name="h2", align_bytes=64)
+        xh2 = sb.tile([P, WIDE], F32, name="xh2", align_bytes=64)
+        ident = sb.tile([P, P], F32, name="ident")
+        nc.gpsimd.memset(ident[:], 0.0)
+        nc.gpsimd.memset(tab_s[:].bitcast(I32), 0)
+        make_identity(nc, ident[:], nomemset=True)
+        nc.vector.memset(h2[:], 0.0)
+        nc.vector.memset(dtab_s[:].bitcast(I32), 0)
+        nc.vector.memset(xh2[:, J:], 0.0)
+        s1 = sb.tile([P, M], F32, name="s1", tag="s1")
+        xs1 = sb.tile([P, M], F32, name="xs1")
+        nc.vector.memset(s1[:], 0.0)
+        nc.vector.memset(xs1[:], 0.0)
+
+        nc.sync.dma_start(idx[:], offs)
+        nc.sync.dma_start(idx2[:], offs2)
+        nc.sync.dma_start(idx3[:], offs3)
+        tab_w = sb.tile([P, T], I32, name="tab_w", tag="tab_w", align_bytes=64)
+        nc.sync.dma_start(tab_w[:], tab_words[0].rearrange("p n t -> p (n t)").bitcast(I32))
+
+        def load_scales(queue, tile, scales):
+            for q in range(4):
+                queue.dma_start(tile[32 * q:32 * q + 4, :].bitcast(I32), scales[0, 4 * q:4 * q + 4, :].bitcast(I32))
+
+        load_scales(nc.scalar, tab_s, tab_scales)
+        warm = sb.tile([P, 1], F32, name="warm")
+        nc.scalar.activation(warm[:], h2[:, J:J + 1], ACT.Tanh)
+        nc.sync.dma_start(h2[:, :PACK * R], w1.rearrange("(p t) r -> p (t r)", t=PACK))
+        load_scales(nc.sync, dtab_s, dtab_scales)
+        pb_c = xh2[:, J:J + PACK]
+        gain_c = xh2[:, J + 8:J + 9]
+        mix_c = xh2[:, J + 16:J + 17]
+        og_c = xh2[:, J + 24:J + 25]
+        nc.sync.dma_start(pb_c, pb.rearrange("o (p c) -> p (o c)", c=PACK))
+        nc.sync.dma_start(gain_c, gain)
+        nc.sync.dma_start(mix_c, mix)
+        nc.sync.dma_start(og_c, og)
+
+        dtab_w = sb.tile([P, T], I32, name="dtab_w", align_bytes=64)
+        nc.gpsimd.dma_start(dtab_w[:], dtab_words[0].rearrange("p n t -> p (n t)").bitcast(I32))
+
+        def quantise(raw, width, name):
+            grouped = sb.tile([P, width, PACK], BF16, name=name + "_bf", tag=name + "_bf", align_bytes=64)
+            nc.scalar.copy(grouped[:], raw.rearrange("p (t w) -> p w t", t=PACK))
+            codes = sb.tile([P, width], U32, name=name + "_codes", align_bytes=64)
+            scales = sb.tile([P, width], U8, name=name + "_scales", align_bytes=64)
+            nc.vector.quantize_mx(out=codes[:].bitcast(FP8X4), scales=scales[:],
+                                  in_=grouped[:].rearrange("p w t -> p (w t)"))
+            return codes, scales
+
+        def gather(window, dtype, name, tag):
+            picked = sb.tile([P, J], dtype, name=name, tag=tag, align_bytes=64)
+            nc.vector.tensor_copy(picked[:], window.indirect(idx[:]))
+            return picked
+
+        def product(acc, lhs, rhs):
+            nc.tensor.matmul_mx(out=acc, lhsT=lhs[0][:].bitcast(FP8X4), lhsT_scale=lhs[1][:],
+                                rhs=rhs[0][:].bitcast(FP8X4), rhs_scale=rhs[1][:], start=True, stop=True)
+
+        g_tab_s = gather(tab_s[:], U8, "g_tab_s", "picked_s")
+        g_tab_w = gather(tab_w[:].bitcast(U32), U32, "g_tab_w", "tab_s")
+        w1q = quantise(h2[:, :PACK * R], R, "w1")
+        a = psum.tile([P, J], F32, name="a", tag="a")
+        product(a[:], w1q, (g_tab_w, g_tab_s))
+        h1 = sb.tile([P, J], F32, name="h1")
+        nc.scalar.activation(h1[:], a[:], ACT.Tanh)
+        nc.scalar.activation(h2[:, :J], h1[:], ACT.Copy, scale=gain_c)
+
+        g_dtab_s = gather(dtab_s[:], U8, "g_dtab_s", "picked_s")
+        g_dtab_w = gather(dtab_w[:].bitcast(U32), U32, "g_dtab_w", "dtab_s")
+        ta = psum.tile([P, J], F32, name="ta")
+        product(ta[:], w1q, (g_dtab_w, g_dtab_s))
+
+        pb_ps = psum.tile([P, PACK, P], F32, name="pb_ps", tag="pb_ps")
+        for c in range(PACK):
+            nc.tensor.transpose(pb_ps[:, c, :], pb_c[:, c:c + 1].to_broadcast([P, P]), ident[:])
+        pb_all = sb.tile([P, P, PACK], F32, name="pb_all")
+        nc.scalar.copy(pb_all[:], pb_ps[:].rearrange("q c p -> q p c"))
+
+        s = sb.tile([P, M], F32, name="s")
+        nc.vector.tensor_tensor(s[:], h2[:].indirect(idx2[:]), pb_all[:].rearrange("q p c -> q (p c)"), ADD)
+
+        sq = sb.tile([P, J], F32, name="sq")
+        nc.scalar.activation(sq[:], h1[:], ACT.Square)
+        om = sb.tile([P, J], F32, name="om")
+        nc.scalar.activation(om[:], sq[:], ACT.Copy, bias=1.0, scale=-1.0)
+
+        s_n = sb.tile([P, N], F32, name="s_n")
+        nc.vector.tensor_copy(s_n[:], s[:].indirect(idx3[:]))
+        v1 = sb.tile([P, N], F32, name="v1")
+        nc.scalar.activation(v1[:], s_n[:], ACT.Copy, scale=mix_c)
+        th = sb.tile([P, N], F32, name="th")
+        nc.scalar.activation(th[:], v1[:], ACT.Tanh, scale=0.5)
+        q4 = sb.tile([P, N], F32, name="q4")
+        nc.scalar.activation(q4[:], th[:], ACT.Square, scale=0.5)
+        sig = sb.tile([P, N], F32, name="sig")
+        nc.scalar.activation(sig[:], th[:], ACT.Copy, bias=0.5, scale=0.5)
+        qn = sb.tile([P, N], F32, name="qn")
+        nc.scalar.activation(qn[:], q4[:], ACT.Copy, bias=-0.25, scale=1.0)
+
+        stage2 = sb.tile([P, PACK * (R + N)], F32, name="stage2", tag="w1_bf", align_bytes=64)
+        nc.sync.dma_start(stage2[:, :PACK * R], wo.rearrange("(p t) r -> p (t r)", t=PACK))
+        nc.sync.dma_start(stage2[:, PACK * R:], dy.rearrange("(p t) n -> p (t n)", t=PACK))
+        base_sb = sb.tile([P, J], F32, name="base_sb", tag="tab_w", align_bytes=64)
+        nc.sync.dma_start(base_sb[:], base)
+        woq = quantise(stage2[:, :PACK * R], R, "wo")
+        dyq = quantise(stage2[:, PACK * R:], N, "dy")
+        c0 = psum.tile([P, N], F32, name="c0", tag="a")
+        product(c0[:], woq, dyq)
+        co = sb.tile([P, N], F32, name="co")
+        nc.scalar.activation(co[:], c0[:], ACT.Copy, scale=og_c)
+        cm = sb.tile([P, N], F32, name="cm")
+        nc.scalar.activation(cm[:], co[:], ACT.Copy, scale=mix_c)
+        cm2 = sb.tile([P, N], F32, name="cm2")
+        nc.scalar.activation(cm2[:], cm[:], ACT.Copy, scale=mix_c)
+
+        nc.vector.scalar_tensor_tensor(xh2[:, :J], ta[:], gain_c, om[:], MULT, MULT)
+        xs = sb.tile([P, M], F32, name="xs")
+        nc.vector.tensor_copy(xs[:], xh2[:].indirect(idx2[:]))
+
+        a1 = sb.tile([P, N], F32, name="a1")
+        nc.vector.tensor_tensor(a1[:], qn[:], v1[:], MULT)
+        b1 = sb.tile([P, N], F32, name="b1")
+        nc.vector.tensor_tensor(b1[:], v1[:], th[:], MULT)
+        f1 = sb.tile([P, N], F32, name="f1")
+        nc.vector.tensor_tensor(f1[:], sig[:], a1[:], SUB)
+        f2 = sb.tile([P, N], F32, name="f2")
+        nc.vector.scalar_tensor_tensor(f2[:], b1[:], 2.0, qn[:], SUB, MULT)
+        nc.vector.tensor_tensor(s1[:].indirect(idx3[:]), f1[:], cm[:], MULT)
+        y = sb.tile([P, N], F32, name="y")
+        nc.vector.tensor_tensor(y[:], xs[:].indirect(idx3[:]), cm2[:], MULT)
+
+        blocks = [slice(c * P, (c + 1) * P) for c in range(J // P)]
+        turned = [psum.tile([P, P], F32, name="turned%d" % c) for c in range(J // P)]
+        for c, cols in enumerate(blocks):
+            nc.tensor.matmul(turned[c][:], base_sb[:, cols], ident[:], start=True, stop=False, is_transpose=True)
+
+        z1 = sb.tile([P, WIDE], F32, name="z1")
+        nc.vector.tensor_tensor(z1[:].indirect(idx2[:]), s1[:], xs[:], MULT)
+        nc.vector.tensor_tensor(xs1[:].indirect(idx3[:]), y[:], f2[:], MULT)
+        t1 = sb.tile([P, J], F32, name="t1")
+        nc.vector.scalar_tensor_tensor(t1[:], z1[:, :J], -2.0, h1[:], MULT, MULT)
+        xs2 = sb.tile([P, WIDE], F32, name="xs2", tag="s1")
+        nc.vector.tensor_copy(xs2[:].indirect(idx2[:]), xs1[:])
+
+        turned_sb = sb.tile([P, J], F32, name="turned_sb")
+        t1b = psum.tile([P, J], F32, name="t1b", tag="pb_ps")
+        for c, cols in enumerate(blocks):
+            nc.tensor.matmul(turned[c][:], t1[:, cols], ident[:], start=False, stop=True, is_transpose=True)
+        for c, cols in enumerate(blocks):
+            nc.scalar.copy(turned_sb[:, cols], turned[c][:])
+            nc.tensor.transpose(t1b[:, cols], turned_sb[:, cols], ident[:])
+
+        t2 = sb.tile([P, J], F32, name="t2")
+        res = sb.tile([P, J], F32, name="res")
+        halves = [slice(0, J // 2), slice(J // 2, J)]
+        for h in halves:
+            nc.vector.scalar_tensor_tensor(t2[:, h], xs2[:, h], gain_c, om[:, h], MULT, MULT)
+        for h in halves:
+            nc.vector.tensor_tensor(res[:, h], t2[:, h], t1b[:, h], ADD)
+            nc.sync.dma_start(out[:, h], res[:, h])

@@ -1,7 +1,6 @@
 from contextlib import ExitStack
 
 import concourse.mybir as mybir
-from concourse.masks import make_identity
 
 K, R, F, T, J, M, N = 512, 128, 512, 2048, 512, 512, 64
 FLOPS = 2 * (2 * K * R * J + F * R * N)
@@ -40,11 +39,15 @@ def tile_attend_hvtwohops_kernel(tc, tab_words, tab_scales, w1, gain, pb, mix, w
         h2 = sb.tile([P, WIDE], F32, name="h2", align_bytes=64)
         xh2 = sb.tile([P, WIDE], F32, name="xh2", align_bytes=64)
         ident = sb.tile([P, P], F32, name="ident")
-        nc.gpsimd.memset(ident[:], 0.0)
+        zeros = sb.tile([P, P], F32, name="zeros", tag="dtab_w", align_bytes=64)
+        nc.gpsimd.memset(zeros[:], 0.0)
         nc.gpsimd.memset(tab_s[:].bitcast(I32), 0)
-        make_identity(nc, ident[:], nomemset=True)
+        nc.gpsimd.affine_select(out=ident[:], in_=zeros[:], pattern=[[-1, P]], compare_op=mybir.AluOpType.not_equal,
+                                fill=1.0, base=0, channel_multiplier=1)
+        nc.gpsimd.memset(dtab_s[:].bitcast(I32), 0)
+        gain_c = sb.tile([P, 1], F32, name="gain_c")[:]
+        nc.gpsimd.dma_start(gain_c, gain)
         nc.vector.memset(h2[:], 0.0)
-        nc.vector.memset(dtab_s[:].bitcast(I32), 0)
         nc.vector.memset(xh2[:, J:], 0.0)
         s1 = sb.tile([P, M], F32, name="s1", tag="s1")
         xs1 = sb.tile([P, M], F32, name="xs1")
@@ -61,113 +64,119 @@ def tile_attend_hvtwohops_kernel(tc, tab_words, tab_scales, w1, gain, pb, mix, w
             for q in range(4):
                 queue.dma_start(tile[32 * q:32 * q + 4, :].bitcast(I32), scales[0, 4 * q:4 * q + 4, :].bitcast(I32))
 
-        load_scales(nc.scalar, tab_s, tab_scales)
+        load_scales(nc.sync, tab_s, tab_scales)
         warm = sb.tile([P, 1], F32, name="warm")
         nc.scalar.activation(warm[:], h2[:, J:J + 1], ACT.Tanh)
         nc.sync.dma_start(h2[:, :PACK * R], w1.rearrange("(p t) r -> p (t r)", t=PACK))
-        load_scales(nc.sync, dtab_s, dtab_scales)
         pb_c = xh2[:, J:J + PACK]
-        gain_c = xh2[:, J + 8:J + 9]
-        mix_c = xh2[:, J + 16:J + 17]
-        og_c = xh2[:, J + 24:J + 25]
         nc.sync.dma_start(pb_c, pb.rearrange("o (p c) -> p (o c)", c=PACK))
-        nc.sync.dma_start(gain_c, gain)
-        nc.sync.dma_start(mix_c, mix)
-        nc.sync.dma_start(og_c, og)
+        dtab_w = sb.tile([P, T], I32, name="dtab_w", tag="dtab_w", align_bytes=64)
+        nc.sync.dma_start(dtab_w[:], dtab_words[0].rearrange("p n t -> p (n t)").bitcast(I32))
 
-        dtab_w = sb.tile([P, T], I32, name="dtab_w", align_bytes=64)
-        nc.gpsimd.dma_start(dtab_w[:], dtab_words[0].rearrange("p n t -> p (n t)").bitcast(I32))
+        load_scales(nc.sync, dtab_s, dtab_scales)
 
-        def quantise(raw, width, name):
-            grouped = sb.tile([P, width, PACK], BF16, name=name + "_bf", tag=name + "_bf", align_bytes=64)
-            nc.scalar.copy(grouped[:], raw.rearrange("p (t w) -> p w t", t=PACK))
-            codes = sb.tile([P, width], U32, name=name + "_codes", align_bytes=64)
+        def quantise(raw, width, name, grouped, codes_tag):
+            nc.scalar.copy(grouped.rearrange("p (w t) -> p w t", t=PACK), raw.rearrange("p (t w) -> p w t", t=PACK))
+            codes = sb.tile([P, width], U32, name=name + "_codes", tag=codes_tag, align_bytes=64)
             scales = sb.tile([P, width], U8, name=name + "_scales", align_bytes=64)
             nc.vector.quantize_mx(out=codes[:].bitcast(FP8X4), scales=scales[:],
-                                  in_=grouped[:].rearrange("p w t -> p (w t)"))
-            return codes, scales
-
-        def gather(window, dtype, name, tag):
-            picked = sb.tile([P, J], dtype, name=name, tag=tag, align_bytes=64)
-            nc.vector.tensor_copy(picked[:], window.indirect(idx[:]))
-            return picked
+                                  in_=grouped)
+            return codes[:], scales[:]
 
         def product(acc, lhs, rhs):
-            nc.tensor.matmul_mx(out=acc, lhsT=lhs[0][:].bitcast(FP8X4), lhsT_scale=lhs[1][:],
-                                rhs=rhs[0][:].bitcast(FP8X4), rhs_scale=rhs[1][:], start=True, stop=True)
+            nc.tensor.matmul_mx(out=acc, lhsT=lhs[0].bitcast(FP8X4), lhsT_scale=lhs[1],
+                                rhs=rhs[0].bitcast(FP8X4), rhs_scale=rhs[1], start=True, stop=True)
 
-        g_tab_s = gather(tab_s[:], U8, "g_tab_s", "picked_s")
-        g_tab_w = gather(tab_w[:].bitcast(U32), U32, "g_tab_w", "tab_s")
-        w1q = quantise(h2[:, :PACK * R], R, "w1")
-        a = psum.tile([P, J], F32, name="a", tag="a")
-        product(a[:], w1q, (g_tab_w, g_tab_s))
-        h1 = sb.tile([P, J], F32, name="h1")
-        nc.scalar.activation(h1[:], a[:], ACT.Tanh)
-        nc.scalar.activation(h2[:, :J], h1[:], ACT.Copy, scale=gain_c)
-
-        g_dtab_s = gather(dtab_s[:], U8, "g_dtab_s", "picked_s")
-        g_dtab_w = gather(dtab_w[:].bitcast(U32), U32, "g_dtab_w", "dtab_s")
-        ta = psum.tile([P, J], F32, name="ta")
-        product(ta[:], w1q, (g_dtab_w, g_dtab_s))
+        halves = [slice(0, J // 2), slice(J // 2, J)]
 
         pb_ps = psum.tile([P, PACK, P], F32, name="pb_ps", tag="pb_ps")
         for c in range(PACK):
             nc.tensor.transpose(pb_ps[:, c, :], pb_c[:, c:c + 1].to_broadcast([P, P]), ident[:])
-        pb_all = sb.tile([P, P, PACK], F32, name="pb_all")
-        nc.scalar.copy(pb_all[:], pb_ps[:].rearrange("q c p -> q p c"))
 
-        s = sb.tile([P, M], F32, name="s")
+        g_tab_w = sb.tile([P, J], U32, name="g_tab_w", tag="g_tab_w", align_bytes=64)
+        nc.vector.tensor_copy(g_tab_w[:], tab_w[:].bitcast(U32).indirect(idx[:]))
+        g_tab_s = sb.tile([P, J], U8, name="g_tab_s", align_bytes=64)
+        nc.vector.tensor_copy(g_tab_s[:], tab_s[:].indirect(idx[:]))
+        w1_bf = sb.tile([P, PACK * R], BF16, name="w1_bf", tag="w1_bf", align_bytes=64)
+        w1q = quantise(h2[:, :PACK * R], R, "w1", w1_bf[:], "w1_codes")
+        pb_all = sb.tile([P, P, PACK], F32, name="pb_all", tag="pb_all", align_bytes=64)
+        nc.scalar.copy(pb_all[:], pb_ps[:].rearrange("q c p -> q p c"))
+        h1 = sb.tile([P, J], F32, name="h1")
+        a = psum.tile([P, J], F32, name="a", tag="a0")
+        product(a[:], w1q, (g_tab_w[:], g_tab_s[:]))
+        nc.scalar.activation(h1[:], a[:], ACT.Tanh)
+        nc.scalar.activation(h2[:, :J], h1[:], ACT.Copy, scale=gain_c)
+
+        g_dtab_w = sb.tile([P, J], U32, name="g_dtab_w", tag="w1_bf", align_bytes=64)
+        nc.vector.tensor_copy(g_dtab_w[:], dtab_w[:].bitcast(U32).indirect(idx[:]))
+        g_dtab_s = sb.tile([P, J], U8, name="g_dtab_s", tag="late", align_bytes=64)
+        nc.vector.tensor_copy(g_dtab_s[:], dtab_s[:].indirect(idx[:]))
+        ta = psum.tile([P, J], F32, name="ta")
+        product(ta[:], w1q, (g_dtab_w[:], g_dtab_s[:]))
+
+        s = sb.tile([P, M], F32, name="s", tag="dtab_w", align_bytes=64)
         nc.vector.tensor_tensor(s[:], h2[:].indirect(idx2[:]), pb_all[:].rearrange("q p c -> q (p c)"), ADD)
 
-        sq = sb.tile([P, J], F32, name="sq")
+        sq = sb.tile([P, J], F32, name="sq", tag="sq", align_bytes=64)
         nc.scalar.activation(sq[:], h1[:], ACT.Square)
         om = sb.tile([P, J], F32, name="om")
         nc.scalar.activation(om[:], sq[:], ACT.Copy, bias=1.0, scale=-1.0)
 
-        s_n = sb.tile([P, N], F32, name="s_n")
-        nc.vector.tensor_copy(s_n[:], s[:].indirect(idx3[:]))
+
+        stage2 = sb.tile([P, PACK * (R + N) + 16], F32, name="stage2", tag="tab_s", align_bytes=64)
+        mix_c = stage2[:, PACK * (R + N):PACK * (R + N) + 1]
+        og_c = stage2[:, PACK * (R + N) + 8:PACK * (R + N) + 9]
+        nc.sync.dma_start(mix_c, mix)
+        nc.sync.dma_start(og_c, og)
+        nc.sync.dma_start(stage2[:, :PACK * R], wo.rearrange("(p t) r -> p (t r)", t=PACK))
+        nc.sync.dma_start(stage2[:, PACK * R:PACK * (R + N)], dy.rearrange("(p t) n -> p (t n)", t=PACK))
+
+        mix_n = sb.tile([P, N], F32, name="mix_n")
+        nc.scalar.copy(mix_n[:], mix_c.to_broadcast([P, N]))
+        factors = sb.tile([P, 2], F32, name="factors")
+        mix_og, mix2_og = factors[:, 0:1], factors[:, 1:2]
+        nc.scalar.activation(mix_og, mix_c, ACT.Copy, scale=og_c)
+        last_bf = sb.tile([P, PACK * (R + N)], BF16, name="last_bf", tag="sq", align_bytes=64)
+        woq = quantise(stage2[:, :PACK * R], R, "wo", last_bf[:, :PACK * R], "late")
+        nc.scalar.activation(mix2_og, mix_og, ACT.Copy, scale=mix_c)
+        dyq = quantise(stage2[:, PACK * R:PACK * (R + N)], N, "dy", last_bf[:, PACK * R:], "dy_codes")
+
         v1 = sb.tile([P, N], F32, name="v1")
-        nc.scalar.activation(v1[:], s_n[:], ACT.Copy, scale=mix_c)
+        nc.vector.tensor_tensor(v1[:], s[:].indirect(idx3[:]), mix_n[:], MULT)
         th = sb.tile([P, N], F32, name="th")
         nc.scalar.activation(th[:], v1[:], ACT.Tanh, scale=0.5)
         q4 = sb.tile([P, N], F32, name="q4")
         nc.scalar.activation(q4[:], th[:], ACT.Square, scale=0.5)
         sig = sb.tile([P, N], F32, name="sig")
         nc.scalar.activation(sig[:], th[:], ACT.Copy, bias=0.5, scale=0.5)
+
+        c0 = psum.tile([P, N], F32, name="c0", tag="a0")
+        product(c0[:], woq, dyq)
+        base_sb = sb.tile([P, J], F32, name="base_sb", tag="late", align_bytes=64)
+        nc.sync.dma_start(base_sb[:], base)
+        cm2 = sb.tile([P, N], F32, name="cm2")
+        nc.scalar.activation(cm2[:], c0[:], ACT.Copy, scale=mix2_og)
+        cm = sb.tile([P, N], F32, name="cm")
+        nc.scalar.activation(cm[:], c0[:], ACT.Copy, scale=mix_og)
+
         qn = sb.tile([P, N], F32, name="qn")
         nc.scalar.activation(qn[:], q4[:], ACT.Copy, bias=-0.25, scale=1.0)
 
-        stage2 = sb.tile([P, PACK * (R + N)], F32, name="stage2", tag="w1_bf", align_bytes=64)
-        nc.sync.dma_start(stage2[:, :PACK * R], wo.rearrange("(p t) r -> p (t r)", t=PACK))
-        nc.sync.dma_start(stage2[:, PACK * R:], dy.rearrange("(p t) n -> p (t n)", t=PACK))
-        base_sb = sb.tile([P, J], F32, name="base_sb", tag="tab_w", align_bytes=64)
-        nc.sync.dma_start(base_sb[:], base)
-        woq = quantise(stage2[:, :PACK * R], R, "wo")
-        dyq = quantise(stage2[:, PACK * R:], N, "dy")
-        c0 = psum.tile([P, N], F32, name="c0", tag="a")
-        product(c0[:], woq, dyq)
-        co = sb.tile([P, N], F32, name="co")
-        nc.scalar.activation(co[:], c0[:], ACT.Copy, scale=og_c)
-        cm = sb.tile([P, N], F32, name="cm")
-        nc.scalar.activation(cm[:], co[:], ACT.Copy, scale=mix_c)
-        cm2 = sb.tile([P, N], F32, name="cm2")
-        nc.scalar.activation(cm2[:], cm[:], ACT.Copy, scale=mix_c)
-
         nc.vector.scalar_tensor_tensor(xh2[:, :J], ta[:], gain_c, om[:], MULT, MULT)
-        xs = sb.tile([P, M], F32, name="xs")
+        xs = sb.tile([P, M], F32, name="xs", tag="sq", align_bytes=64)
         nc.vector.tensor_copy(xs[:], xh2[:].indirect(idx2[:]))
 
         a1 = sb.tile([P, N], F32, name="a1")
-        nc.vector.tensor_tensor(a1[:], qn[:], v1[:], MULT)
+        nc.vector.scalar_tensor_tensor(a1[:], q4[:], 0.25, v1[:], SUB, MULT)
         b1 = sb.tile([P, N], F32, name="b1")
         nc.vector.tensor_tensor(b1[:], v1[:], th[:], MULT)
         f1 = sb.tile([P, N], F32, name="f1")
         nc.vector.tensor_tensor(f1[:], sig[:], a1[:], SUB)
-        f2 = sb.tile([P, N], F32, name="f2")
-        nc.vector.scalar_tensor_tensor(f2[:], b1[:], 2.0, qn[:], SUB, MULT)
-        nc.vector.tensor_tensor(s1[:].indirect(idx3[:]), f1[:], cm[:], MULT)
         y = sb.tile([P, N], F32, name="y")
         nc.vector.tensor_tensor(y[:], xs[:].indirect(idx3[:]), cm2[:], MULT)
+        nc.vector.tensor_tensor(s1[:].indirect(idx3[:]), f1[:], cm[:], MULT)
+        c1 = sb.tile([P, N], F32, name="c1")
+        nc.vector.scalar_tensor_tensor(c1[:], b1[:], 2.0, y[:], SUB, MULT)
 
         blocks = [slice(c * P, (c + 1) * P) for c in range(J // P)]
         turned = [psum.tile([P, P], F32, name="turned%d" % c) for c in range(J // P)]
@@ -176,7 +185,7 @@ def tile_attend_hvtwohops_kernel(tc, tab_words, tab_scales, w1, gain, pb, mix, w
 
         z1 = sb.tile([P, WIDE], F32, name="z1")
         nc.vector.tensor_tensor(z1[:].indirect(idx2[:]), s1[:], xs[:], MULT)
-        nc.vector.tensor_tensor(xs1[:].indirect(idx3[:]), y[:], f2[:], MULT)
+        nc.vector.tensor_tensor(xs1[:].indirect(idx3[:]), c1[:], qn[:], MULT)
         t1 = sb.tile([P, J], F32, name="t1")
         nc.vector.scalar_tensor_tensor(t1[:], z1[:, :J], -2.0, h1[:], MULT, MULT)
         xs2 = sb.tile([P, WIDE], F32, name="xs2", tag="s1")
@@ -192,7 +201,6 @@ def tile_attend_hvtwohops_kernel(tc, tab_words, tab_scales, w1, gain, pb, mix, w
 
         t2 = sb.tile([P, J], F32, name="t2")
         res = sb.tile([P, J], F32, name="res")
-        halves = [slice(0, J // 2), slice(J // 2, J)]
         for h in halves:
             nc.vector.scalar_tensor_tensor(t2[:, h], xs2[:, h], gain_c, om[:, h], MULT, MULT)
         for h in halves:

@@ -20,6 +20,7 @@ SUB = mybir.AluOpType.subtract
 P = 128
 PACK = 4
 WIDE = 704
+XWIDE = 800
 
 
 def tile_attend_hvtwohops_kernel(tc, tab_words, tab_scales, w1, gain, pb, mix, wo, dy, dtab_words, dtab_scales,
@@ -37,7 +38,7 @@ def tile_attend_hvtwohops_kernel(tc, tab_words, tab_scales, w1, gain, pb, mix, w
         tab_s = sb.tile([P, T], U8, name="tab_s", tag="tab_s", align_bytes=64)
         dtab_s = sb.tile([P, T], U8, name="dtab_s", tag="dtab_s", align_bytes=64)
         h2 = sb.tile([P, WIDE], F32, name="h2", align_bytes=64)
-        xh2 = sb.tile([P, WIDE], F32, name="xh2", align_bytes=64)
+        xh2 = sb.tile([P, XWIDE], F32, name="xh2", align_bytes=64)
         ident = sb.tile([P, P], F32, name="ident")
         zeros = sb.tile([P, P], F32, name="zeros", tag="dtab_w", align_bytes=64)
         nc.gpsimd.memset(zeros[:], 0.0)
@@ -45,10 +46,8 @@ def tile_attend_hvtwohops_kernel(tc, tab_words, tab_scales, w1, gain, pb, mix, w
         nc.gpsimd.affine_select(out=ident[:], in_=zeros[:], pattern=[[-1, P]], compare_op=mybir.AluOpType.not_equal,
                                 fill=1.0, base=0, channel_multiplier=1)
         nc.gpsimd.memset(dtab_s[:].bitcast(I32), 0)
-        gain_c = sb.tile([P, 1], F32, name="gain_c")[:]
-        nc.gpsimd.dma_start(gain_c, gain)
+        nc.gpsimd.memset(xh2[:], 0.0)
         nc.vector.memset(h2[:], 0.0)
-        nc.vector.memset(xh2[:, J:], 0.0)
         s1 = sb.tile([P, M], F32, name="s1", tag="s1")
         xs1 = sb.tile([P, M], F32, name="xs1")
         nc.vector.memset(s1[:], 0.0)
@@ -65,15 +64,21 @@ def tile_attend_hvtwohops_kernel(tc, tab_words, tab_scales, w1, gain, pb, mix, w
                 queue.dma_start(tile[32 * q:32 * q + 4, :].bitcast(I32), scales[0, 4 * q:4 * q + 4, :].bitcast(I32))
 
         load_scales(nc.sync, tab_s, tab_scales)
-        warm = sb.tile([P, 1], F32, name="warm")
-        nc.scalar.activation(warm[:], h2[:, J:J + 1], ACT.Tanh)
         nc.sync.dma_start(h2[:, :PACK * R], w1.rearrange("(p t) r -> p (t r)", t=PACK))
-        pb_c = xh2[:, J:J + PACK]
+        pb_c = h2[:, J + 8:J + 8 + PACK]
         nc.sync.dma_start(pb_c, pb.rearrange("o (p c) -> p (o c)", c=PACK))
         dtab_w = sb.tile([P, T], I32, name="dtab_w", tag="dtab_w", align_bytes=64)
         nc.sync.dma_start(dtab_w[:], dtab_words[0].rearrange("p n t -> p (n t)").bitcast(I32))
 
         load_scales(nc.sync, dtab_s, dtab_scales)
+        wo_raw = xh2[:, :PACK * R]
+        dy_raw = xh2[:, J:J + PACK * N]
+        gain_c, mix_c, og_c = (xh2[:, c:c + 1] for c in range(J + PACK * N, J + PACK * N + 24, 8))
+        nc.sync.dma_start(gain_c, gain)
+        nc.sync.dma_start(wo_raw, wo.rearrange("(p t) r -> p (t r)", t=PACK))
+        nc.sync.dma_start(dy_raw, dy.rearrange("(p t) n -> p (t n)", t=PACK))
+        nc.sync.dma_start(mix_c, mix)
+        nc.sync.dma_start(og_c, og)
 
         def quantise(raw, width, name, grouped, codes_tag):
             nc.scalar.copy(grouped.rearrange("p (w t) -> p w t", t=PACK), raw.rearrange("p (t w) -> p w t", t=PACK))
@@ -95,7 +100,7 @@ def tile_attend_hvtwohops_kernel(tc, tab_words, tab_scales, w1, gain, pb, mix, w
 
         g_tab_w = sb.tile([P, J], U32, name="g_tab_w", tag="g_tab_w", align_bytes=64)
         nc.vector.tensor_copy(g_tab_w[:], tab_w[:].bitcast(U32).indirect(idx[:]))
-        g_tab_s = sb.tile([P, J], U8, name="g_tab_s", align_bytes=64)
+        g_tab_s = sb.tile([P, J], U8, name="g_tab_s", tag="late", align_bytes=64)
         nc.vector.tensor_copy(g_tab_s[:], tab_s[:].indirect(idx[:]))
         w1_bf = sb.tile([P, PACK * R], BF16, name="w1_bf", tag="w1_bf", align_bytes=64)
         w1q = quantise(h2[:, :PACK * R], R, "w1", w1_bf[:], "w1_codes")
@@ -117,32 +122,27 @@ def tile_attend_hvtwohops_kernel(tc, tab_words, tab_scales, w1, gain, pb, mix, w
         s = sb.tile([P, M], F32, name="s", tag="dtab_w", align_bytes=64)
         nc.vector.tensor_tensor(s[:], h2[:].indirect(idx2[:]), pb_all[:].rearrange("q p c -> q (p c)"), ADD)
 
-        sq = sb.tile([P, J], F32, name="sq", tag="sq", align_bytes=64)
-        nc.scalar.activation(sq[:], h1[:], ACT.Square)
         om = sb.tile([P, J], F32, name="om")
-        nc.scalar.activation(om[:], sq[:], ACT.Copy, bias=1.0, scale=-1.0)
+        sq = [sb.tile([P, J // 2], F32, name="sq%d" % u, tag="sq%d" % u, align_bytes=64) for u in range(2)]
+        for u, h in enumerate(halves):
+            nc.scalar.activation(sq[u][:], h1[:, h], ACT.Square)
+        for u, h in enumerate(halves):
+            nc.scalar.activation(om[:, h], sq[u][:], ACT.Copy, bias=1.0, scale=-1.0)
 
-
-        stage2 = sb.tile([P, PACK * (R + N) + 16], F32, name="stage2", tag="tab_s", align_bytes=64)
-        mix_c = stage2[:, PACK * (R + N):PACK * (R + N) + 1]
-        og_c = stage2[:, PACK * (R + N) + 8:PACK * (R + N) + 9]
-        nc.sync.dma_start(mix_c, mix)
-        nc.sync.dma_start(og_c, og)
-        nc.sync.dma_start(stage2[:, :PACK * R], wo.rearrange("(p t) r -> p (t r)", t=PACK))
-        nc.sync.dma_start(stage2[:, PACK * R:PACK * (R + N)], dy.rearrange("(p t) n -> p (t n)", t=PACK))
-
-        mix_n = sb.tile([P, N], F32, name="mix_n")
-        nc.scalar.copy(mix_n[:], mix_c.to_broadcast([P, N]))
-        factors = sb.tile([P, 2], F32, name="factors")
-        mix_og, mix2_og = factors[:, 0:1], factors[:, 1:2]
+        stage3 = sb.tile([P, PACK * R // 2 + N + 2], F32, name="stage3", tag="sq0", align_bytes=64)
+        wo_bf = stage3[:, :PACK * R // 2].bitcast(BF16)
+        mix_n = stage3[:, PACK * R // 2:PACK * R // 2 + N]
+        mix_og = stage3[:, PACK * R // 2 + N:PACK * R // 2 + N + 1]
+        mix2_og = stage3[:, PACK * R // 2 + N + 1:]
+        dy_bf = sb.tile([P, PACK * N], BF16, name="dy_bf", tag="sq1", align_bytes=64)
+        woq = quantise(wo_raw, R, "wo", wo_bf, "late")
+        dyq = quantise(dy_raw, N, "dy", dy_bf[:], "dy_codes")
+        nc.scalar.copy(mix_n, mix_c.to_broadcast([P, N]))
         nc.scalar.activation(mix_og, mix_c, ACT.Copy, scale=og_c)
-        last_bf = sb.tile([P, PACK * (R + N)], BF16, name="last_bf", tag="sq", align_bytes=64)
-        woq = quantise(stage2[:, :PACK * R], R, "wo", last_bf[:, :PACK * R], "late")
         nc.scalar.activation(mix2_og, mix_og, ACT.Copy, scale=mix_c)
-        dyq = quantise(stage2[:, PACK * R:PACK * (R + N)], N, "dy", last_bf[:, PACK * R:], "dy_codes")
 
         v1 = sb.tile([P, N], F32, name="v1")
-        nc.vector.tensor_tensor(v1[:], s[:].indirect(idx3[:]), mix_n[:], MULT)
+        nc.vector.tensor_tensor(v1[:], s[:].indirect(idx3[:]), mix_n, MULT)
         th = sb.tile([P, N], F32, name="th")
         nc.scalar.activation(th[:], v1[:], ACT.Tanh, scale=0.5)
         q4 = sb.tile([P, N], F32, name="q4")
@@ -163,7 +163,7 @@ def tile_attend_hvtwohops_kernel(tc, tab_words, tab_scales, w1, gain, pb, mix, w
         nc.scalar.activation(qn[:], q4[:], ACT.Copy, bias=-0.25, scale=1.0)
 
         nc.vector.scalar_tensor_tensor(xh2[:, :J], ta[:], gain_c, om[:], MULT, MULT)
-        xs = sb.tile([P, M], F32, name="xs", tag="sq", align_bytes=64)
+        xs = sb.tile([P, M], F32, name="xs", tag="sq1", align_bytes=64)
         nc.vector.tensor_copy(xs[:], xh2[:].indirect(idx2[:]))
 
         a1 = sb.tile([P, N], F32, name="a1")

@@ -60,10 +60,13 @@ def tile_attend_hvtwohops_kernel(tc, tab_words, tab_scales, w1, gain, pb, mix, w
         nc.sync.dma_start(tab_w[:], tab_words[0].rearrange("p n t -> p (n t)").bitcast(I32))
 
         def load_scales(queue, tile, scales):
-            for q in range(4):
-                queue.dma_start(tile[32 * q:32 * q + 4, :].bitcast(I32), scales[0, 4 * q:4 * q + 4, :].bitcast(I32))
+            rows = scales[0].rearrange("(q r) c -> r q c", r=4)
+            for r in range(4):
+                queue.dma_start(tile[r:P:32, :].bitcast(I32), rows[r].bitcast(I32))
 
         load_scales(nc.sync, tab_s, tab_scales)
+        warm = sb.tile([P, 1], F32, name="warm")
+        nc.scalar.activation(warm[:], h2[:, J:J + 1], ACT.Tanh)
         nc.sync.dma_start(h2[:, :PACK * R], w1.rearrange("(p t) r -> p (t r)", t=PACK))
         pb_c = h2[:, J + 8:J + 8 + PACK]
         nc.sync.dma_start(pb_c, pb.rearrange("o (p c) -> p (o c)", c=PACK))

@@ -19,6 +19,9 @@ SUB = mybir.AluOpType.subtract
 
 P = 128
 PACK = 4
+QUADRANT = 32
+LIST_ROWS = 16
+COLUMN_STEP = 8
 WIDE = 704
 XWIDE = 800
 
@@ -31,9 +34,9 @@ def tile_attend_hvtwohops_kernel(tc, tab_words, tab_scales, w1, gain, pb, mix, w
         sb = ctx.enter_context(tc.tile_pool(name="sb", bufs=1))
         psum = ctx.enter_context(tc.psum_pool(name="psum", bufs=1))
 
-        idx = lists.tile([P, J // 16], U16, name="idx")
-        idx2 = lists.tile([P, M // 16], U16, name="idx2")
-        idx3 = lists.tile([P, N // 16], U16, name="idx3")
+        idx = lists.tile([P, J // LIST_ROWS], U16, name="idx")
+        idx2 = lists.tile([P, M // LIST_ROWS], U16, name="idx2")
+        idx3 = lists.tile([P, N // LIST_ROWS], U16, name="idx3")
 
         tab_s = sb.tile([P, T], U8, name="tab_s", tag="tab_s", align_bytes=64)
         dtab_s = sb.tile([P, T], U8, name="dtab_s", tag="dtab_s", align_bytes=64)
@@ -48,7 +51,7 @@ def tile_attend_hvtwohops_kernel(tc, tab_words, tab_scales, w1, gain, pb, mix, w
         nc.gpsimd.memset(dtab_s[:].bitcast(I32), 0)
         nc.gpsimd.memset(xh2[:], 0.0)
         nc.vector.memset(h2[:], 0.0)
-        s1 = sb.tile([P, M], F32, name="s1", tag="s1")
+        s1 = sb.tile([P, M], F32, name="s1")
         xs1 = sb.tile([P, M], F32, name="xs1")
         nc.vector.memset(s1[:], 0.0)
         nc.vector.memset(xs1[:], 0.0)
@@ -59,24 +62,26 @@ def tile_attend_hvtwohops_kernel(tc, tab_words, tab_scales, w1, gain, pb, mix, w
         tab_w = sb.tile([P, T], I32, name="tab_w", tag="tab_w", align_bytes=64)
         nc.sync.dma_start(tab_w[:], tab_words[0].rearrange("p n t -> p (n t)").bitcast(I32))
 
-        def load_scales(queue, tile, scales):
+        def load_scales(tile, scales):
             rows = scales[0].rearrange("(q r) c -> r q c", r=4)
             for r in range(4):
-                queue.dma_start(tile[r:P:32, :].bitcast(I32), rows[r].bitcast(I32))
+                nc.sync.dma_start(tile[r:P:QUADRANT, :].bitcast(I32), rows[r].bitcast(I32))
 
-        load_scales(nc.sync, tab_s, tab_scales)
+        load_scales(tab_s, tab_scales)
         warm = sb.tile([P, 1], F32, name="warm")
         nc.scalar.activation(warm[:], h2[:, J:J + 1], ACT.Tanh)
-        nc.sync.dma_start(h2[:, :PACK * R], w1.rearrange("(p t) r -> p (t r)", t=PACK))
-        pb_c = h2[:, J + 8:J + 8 + PACK]
+        w1_raw = h2[:, :PACK * R]
+        nc.sync.dma_start(w1_raw, w1.rearrange("(p t) r -> p (t r)", t=PACK))
+        pb_c = h2[:, J + COLUMN_STEP:J + COLUMN_STEP + PACK]
         nc.sync.dma_start(pb_c, pb.rearrange("o (p c) -> p (o c)", c=PACK))
         dtab_w = sb.tile([P, T], I32, name="dtab_w", tag="dtab_w", align_bytes=64)
         nc.sync.dma_start(dtab_w[:], dtab_words[0].rearrange("p n t -> p (n t)").bitcast(I32))
-
-        load_scales(nc.sync, dtab_s, dtab_scales)
+        load_scales(dtab_s, dtab_scales)
         wo_raw = xh2[:, :PACK * R]
         dy_raw = xh2[:, J:J + PACK * N]
-        gain_c, mix_c, og_c = (xh2[:, c:c + 1] for c in range(J + PACK * N, J + PACK * N + 24, 8))
+        first_factor = J + PACK * N
+        gain_c, mix_c, og_c = (xh2[:, c:c + 1]
+                               for c in range(first_factor, first_factor + 3 * COLUMN_STEP, COLUMN_STEP))
         nc.sync.dma_start(gain_c, gain)
         nc.sync.dma_start(wo_raw, wo.rearrange("(p t) r -> p (t r)", t=PACK))
         nc.sync.dma_start(dy_raw, dy.rearrange("(p t) n -> p (t n)", t=PACK))
@@ -87,8 +92,7 @@ def tile_attend_hvtwohops_kernel(tc, tab_words, tab_scales, w1, gain, pb, mix, w
             nc.scalar.copy(grouped.rearrange("p (w t) -> p w t", t=PACK), raw.rearrange("p (t w) -> p w t", t=PACK))
             codes = sb.tile([P, width], U32, name=name + "_codes", tag=codes_tag, align_bytes=64)
             scales = sb.tile([P, width], U8, name=name + "_scales", align_bytes=64)
-            nc.vector.quantize_mx(out=codes[:].bitcast(FP8X4), scales=scales[:],
-                                  in_=grouped)
+            nc.vector.quantize_mx(out=codes[:].bitcast(FP8X4), scales=scales[:], in_=grouped)
             return codes[:], scales[:]
 
         def product(acc, lhs, rhs):
@@ -106,7 +110,7 @@ def tile_attend_hvtwohops_kernel(tc, tab_words, tab_scales, w1, gain, pb, mix, w
         g_tab_s = sb.tile([P, J], U8, name="g_tab_s", tag="late", align_bytes=64)
         nc.vector.tensor_copy(g_tab_s[:], tab_s[:].indirect(idx[:]))
         w1_bf = sb.tile([P, PACK * R], BF16, name="w1_bf", tag="w1_bf", align_bytes=64)
-        w1q = quantise(h2[:, :PACK * R], R, "w1", w1_bf[:], "w1_codes")
+        w1q = quantise(w1_raw, R, "w1", w1_bf[:], "w1_codes")
         pb_all = sb.tile([P, P, PACK], F32, name="pb_all", tag="pb_all", align_bytes=64)
         nc.scalar.copy(pb_all[:], pb_ps[:].rearrange("q c p -> q p c"))
         h1 = sb.tile([P, J], F32, name="h1")
@@ -132,17 +136,20 @@ def tile_attend_hvtwohops_kernel(tc, tab_words, tab_scales, w1, gain, pb, mix, w
         for u, h in enumerate(halves):
             nc.scalar.activation(om[:, h], sq[u][:], ACT.Copy, bias=1.0, scale=-1.0)
 
-        stage3 = sb.tile([P, PACK * R // 2 + N + 2], F32, name="stage3", tag="sq0", align_bytes=64)
-        wo_bf = stage3[:, :PACK * R // 2].bitcast(BF16)
-        mix_n = stage3[:, PACK * R // 2:PACK * R // 2 + N]
-        mix_og = stage3[:, PACK * R // 2 + N:PACK * R // 2 + N + 1]
-        mix2_og = stage3[:, PACK * R // 2 + N + 1:]
+        wo_columns = PACK * R // 2
+        stage3 = sb.tile([P, wo_columns + N + 3], F32, name="stage3", tag="sq0", align_bytes=64)
+        wo_bf = stage3[:, :wo_columns].bitcast(BF16)
+        mix_n = stage3[:, wo_columns:wo_columns + N]
+        mix_og = stage3[:, wo_columns + N:wo_columns + N + 1]
+        mix2_og = stage3[:, wo_columns + N + 1:wo_columns + N + 2]
+        m2_mix_og = stage3[:, wo_columns + N + 2:]
         dy_bf = sb.tile([P, PACK * N], BF16, name="dy_bf", tag="sq1", align_bytes=64)
         woq = quantise(wo_raw, R, "wo", wo_bf, "late")
         dyq = quantise(dy_raw, N, "dy", dy_bf[:], "dy_codes")
         nc.scalar.copy(mix_n, mix_c.to_broadcast([P, N]))
         nc.scalar.activation(mix_og, mix_c, ACT.Copy, scale=og_c)
         nc.scalar.activation(mix2_og, mix_og, ACT.Copy, scale=mix_c)
+        nc.scalar.activation(m2_mix_og, mix_og, ACT.Copy, scale=-2.0)
 
         v1 = sb.tile([P, N], F32, name="v1")
         nc.vector.tensor_tensor(v1[:], s[:].indirect(idx3[:]), mix_n, MULT)
@@ -160,8 +167,7 @@ def tile_attend_hvtwohops_kernel(tc, tab_words, tab_scales, w1, gain, pb, mix, w
         cm2 = sb.tile([P, N], F32, name="cm2")
         nc.scalar.activation(cm2[:], c0[:], ACT.Copy, scale=mix2_og)
         cm = sb.tile([P, N], F32, name="cm")
-        nc.scalar.activation(cm[:], c0[:], ACT.Copy, scale=mix_og)
-
+        nc.scalar.activation(cm[:], c0[:], ACT.Copy, scale=m2_mix_og)
         qn = sb.tile([P, N], F32, name="qn")
         nc.scalar.activation(qn[:], q4[:], ACT.Copy, bias=-0.25, scale=1.0)
 
@@ -173,13 +179,14 @@ def tile_attend_hvtwohops_kernel(tc, tab_words, tab_scales, w1, gain, pb, mix, w
         nc.vector.scalar_tensor_tensor(a1[:], q4[:], 0.25, v1[:], SUB, MULT)
         b1 = sb.tile([P, N], F32, name="b1")
         nc.vector.tensor_tensor(b1[:], v1[:], th[:], MULT)
-        f1 = sb.tile([P, N], F32, name="f1")
-        nc.vector.tensor_tensor(f1[:], sig[:], a1[:], SUB)
         y = sb.tile([P, N], F32, name="y")
         nc.vector.tensor_tensor(y[:], xs[:].indirect(idx3[:]), cm2[:], MULT)
-        nc.vector.tensor_tensor(s1[:].indirect(idx3[:]), f1[:], cm[:], MULT)
+        f1 = sb.tile([P, N], F32, name="f1")
+        nc.vector.tensor_tensor(f1[:], sig[:], a1[:], SUB)
         c1 = sb.tile([P, N], F32, name="c1")
         nc.vector.scalar_tensor_tensor(c1[:], b1[:], 2.0, y[:], SUB, MULT)
+        nc.vector.tensor_tensor(s1[:].indirect(idx3[:]), f1[:], cm[:], MULT)
+        nc.vector.tensor_tensor(xs1[:].indirect(idx3[:]), c1[:], qn[:], MULT)
 
         blocks = [slice(c * P, (c + 1) * P) for c in range(J // P)]
         turned = [psum.tile([P, P], F32, name="turned%d" % c) for c in range(J // P)]
@@ -188,10 +195,10 @@ def tile_attend_hvtwohops_kernel(tc, tab_words, tab_scales, w1, gain, pb, mix, w
 
         z1 = sb.tile([P, WIDE], F32, name="z1")
         nc.vector.tensor_tensor(z1[:].indirect(idx2[:]), s1[:], xs[:], MULT)
-        nc.vector.tensor_tensor(xs1[:].indirect(idx3[:]), c1[:], qn[:], MULT)
         t1 = sb.tile([P, J], F32, name="t1")
-        nc.vector.scalar_tensor_tensor(t1[:], z1[:, :J], -2.0, h1[:], MULT, MULT)
-        xs2 = sb.tile([P, WIDE], F32, name="xs2", tag="s1")
+        for h in halves:
+            nc.gpsimd.tensor_tensor(t1[:, h], z1[:, h], h1[:, h], MULT)
+        xs2 = sb.tile([P, WIDE], F32, name="xs2")
         nc.vector.tensor_copy(xs2[:].indirect(idx2[:]), xs1[:])
 
         turned_sb = sb.tile([P, J], F32, name="turned_sb")

from contextlib import ExitStack

import concourse.mybir as mybir

K, R, F, T, J, M, N = 512, 128, 512, 2048, 512, 512, 64
FLOPS = 2 * (2 * K * R * J + F * R * N)

F32 = mybir.dt.float32
BF16 = mybir.dt.bfloat16
I32 = mybir.dt.int32
U32 = mybir.dt.uint32
U16 = mybir.dt.uint16
U8 = mybir.dt.uint8
FP8X4 = mybir.dt.float8_e4m3fn_x4
ACT = mybir.ActivationFunctionType
MULT = mybir.AluOpType.mult
ADD = mybir.AluOpType.add
SUB = mybir.AluOpType.subtract

P = 128
PACK = 4
QUADRANT = 32
LIST_ROWS = 16
COLUMN_STEP = 8
WIDE = 704
XWIDE = 800


def tile_attend_hvtwohops_kernel(tc, tab_words, tab_scales, w1, gain, pb, mix, wo, dy, dtab_words, dtab_scales,
                                  og, base, offs, offs2, offs3, out):
    nc = tc.nc
    with ExitStack() as ctx:
        lists = ctx.enter_context(tc.tile_pool(name="lists", bufs=1))
        sb = ctx.enter_context(tc.tile_pool(name="sb", bufs=1))
        psum = ctx.enter_context(tc.psum_pool(name="psum", bufs=1))

        idx = lists.tile([P, J // LIST_ROWS], U16, name="idx")
        idx2 = lists.tile([P, M // LIST_ROWS], U16, name="idx2")
        idx3 = lists.tile([P, N // LIST_ROWS], U16, name="idx3")

        tab_s = sb.tile([P, T], U8, name="tab_s", tag="tab_s", align_bytes=64)
        dtab_s = sb.tile([P, T], U8, name="dtab_s", tag="dtab_s", align_bytes=64)
        h2 = sb.tile([P, WIDE], F32, name="h2", align_bytes=64)
        xh2 = sb.tile([P, XWIDE], F32, name="xh2", align_bytes=64)
        ident = sb.tile([P, P], F32, name="ident")
        zeros = sb.tile([P, P], F32, name="zeros", tag="dtab_w", align_bytes=64)
        nc.gpsimd.memset(zeros[:], 0.0)
        nc.gpsimd.memset(tab_s[:].bitcast(I32), 0)
        nc.gpsimd.affine_select(out=ident[:], in_=zeros[:], pattern=[[-1, P]], compare_op=mybir.AluOpType.not_equal,
                                fill=1.0, base=0, channel_multiplier=1)
        nc.gpsimd.memset(dtab_s[:].bitcast(I32), 0)
        nc.gpsimd.memset(xh2[:], 0.0)
        nc.vector.memset(h2[:], 0.0)
        s1 = sb.tile([P, M], F32, name="s1")
        xs1 = sb.tile([P, M], F32, name="xs1")
        nc.vector.memset(s1[:], 0.0)
        nc.vector.memset(xs1[:], 0.0)

        nc.sync.dma_start(idx[:], offs)
        nc.sync.dma_start(idx2[:], offs2)
        nc.sync.dma_start(idx3[:], offs3)
        tab_w = sb.tile([P, T], I32, name="tab_w", tag="tab_w", align_bytes=64)
        nc.sync.dma_start(tab_w[:], tab_words[0].rearrange("p n t -> p (n t)").bitcast(I32))

        def load_scales(tile, scales):
            rows = scales[0].rearrange("(q r) c -> r q c", r=4)
            for r in range(4):
                nc.sync.dma_start(tile[r:P:QUADRANT, :].bitcast(I32), rows[r].bitcast(I32))

        load_scales(tab_s, tab_scales)
        warm = sb.tile([P, 1], F32, name="warm")
        nc.scalar.activation(warm[:], h2[:, J:J + 1], ACT.Tanh)
        w1_raw = h2[:, :PACK * R]
        nc.sync.dma_start(w1_raw, w1.rearrange("(p t) r -> p (t r)", t=PACK))
        pb_c = h2[:, J + COLUMN_STEP:J + COLUMN_STEP + PACK]
        nc.sync.dma_start(pb_c, pb.rearrange("o (p c) -> p (o c)", c=PACK))
        dtab_w = sb.tile([P, T], I32, name="dtab_w", tag="dtab_w", align_bytes=64)
        nc.sync.dma_start(dtab_w[:], dtab_words[0].rearrange("p n t -> p (n t)").bitcast(I32))
        load_scales(dtab_s, dtab_scales)
        wo_raw = xh2[:, :PACK * R]
        dy_raw = xh2[:, J:J + PACK * N]
        first_factor = J + PACK * N
        gain_c, mix_c, og_c = (xh2[:, c:c + 1]
                               for c in range(first_factor, first_factor + 3 * COLUMN_STEP, COLUMN_STEP))
        nc.sync.dma_start(gain_c, gain)
        nc.sync.dma_start(wo_raw, wo.rearrange("(p t) r -> p (t r)", t=PACK))
        nc.sync.dma_start(dy_raw, dy.rearrange("(p t) n -> p (t n)", t=PACK))
        nc.sync.dma_start(mix_c, mix)
        nc.sync.dma_start(og_c, og)

        def quantise(raw, width, name, grouped, codes_tag):
            nc.scalar.copy(grouped.rearrange("p (w t) -> p w t", t=PACK), raw.rearrange("p (t w) -> p w t", t=PACK))
            codes = sb.tile([P, width], U32, name=name + "_codes", tag=codes_tag, align_bytes=64)
            scales = sb.tile([P, width], U8, name=name + "_scales", align_bytes=64)
            nc.vector.quantize_mx(out=codes[:].bitcast(FP8X4), scales=scales[:], in_=grouped)
            return codes[:], scales[:]

        def product(acc, lhs, rhs):
            nc.tensor.matmul_mx(out=acc, lhsT=lhs[0].bitcast(FP8X4), lhsT_scale=lhs[1],
                                rhs=rhs[0].bitcast(FP8X4), rhs_scale=rhs[1], start=True, stop=True)

        halves = [slice(0, J // 2), slice(J // 2, J)]

        pb_ps = psum.tile([P, PACK, P], F32, name="pb_ps", tag="pb_ps")
        for c in range(PACK):
            nc.tensor.transpose(pb_ps[:, c, :], pb_c[:, c:c + 1].to_broadcast([P, P]), ident[:])

        g_tab_w = sb.tile([P, J], U32, name="g_tab_w", tag="g_tab_w", align_bytes=64)
        nc.vector.tensor_copy(g_tab_w[:], tab_w[:].bitcast(U32).indirect(idx[:]))
        g_tab_s = sb.tile([P, J], U8, name="g_tab_s", tag="late", align_bytes=64)
        nc.vector.tensor_copy(g_tab_s[:], tab_s[:].indirect(idx[:]))
        w1_bf = sb.tile([P, PACK * R], BF16, name="w1_bf", tag="w1_bf", align_bytes=64)
        w1q = quantise(w1_raw, R, "w1", w1_bf[:], "w1_codes")
        pb_all = sb.tile([P, P, PACK], F32, name="pb_all", tag="pb_all", align_bytes=64)
        nc.scalar.copy(pb_all[:], pb_ps[:].rearrange("q c p -> q p c"))
        h1 = sb.tile([P, J], F32, name="h1")
        a = psum.tile([P, J], F32, name="a", tag="a0")
        product(a[:], w1q, (g_tab_w[:], g_tab_s[:]))
        nc.scalar.activation(h1[:], a[:], ACT.Tanh)
        nc.scalar.activation(h2[:, :J], h1[:], ACT.Copy, scale=gain_c)

        g_dtab_w = sb.tile([P, J], U32, name="g_dtab_w", tag="w1_bf", align_bytes=64)
        nc.vector.tensor_copy(g_dtab_w[:], dtab_w[:].bitcast(U32).indirect(idx[:]))
        g_dtab_s = sb.tile([P, J], U8, name="g_dtab_s", tag="late", align_bytes=64)
        nc.vector.tensor_copy(g_dtab_s[:], dtab_s[:].indirect(idx[:]))
        ta = psum.tile([P, J], F32, name="ta")
        product(ta[:], w1q, (g_dtab_w[:], g_dtab_s[:]))

        s = sb.tile([P, M], F32, name="s", tag="dtab_w", align_bytes=64)
        nc.vector.tensor_tensor(s[:], h2[:].indirect(idx2[:]), pb_all[:].rearrange("q p c -> q (p c)"), ADD)

        om = sb.tile([P, J], F32, name="om")
        sq = [sb.tile([P, J // 2], F32, name="sq%d" % u, tag="sq%d" % u, align_bytes=64) for u in range(2)]
        for u, h in enumerate(halves):
            nc.scalar.activation(sq[u][:], h1[:, h], ACT.Square)
        for u, h in enumerate(halves):
            nc.scalar.activation(om[:, h], sq[u][:], ACT.Copy, bias=1.0, scale=-1.0)

        wo_columns = PACK * R // 2
        stage3 = sb.tile([P, wo_columns + N + 3], F32, name="stage3", tag="sq0", align_bytes=64)
        wo_bf = stage3[:, :wo_columns].bitcast(BF16)
        mix_n = stage3[:, wo_columns:wo_columns + N]
        mix_og = stage3[:, wo_columns + N:wo_columns + N + 1]
        mix2_og = stage3[:, wo_columns + N + 1:wo_columns + N + 2]
        m2_mix_og = stage3[:, wo_columns + N + 2:]
        dy_bf = sb.tile([P, PACK * N], BF16, name="dy_bf", tag="sq1", align_bytes=64)
        woq = quantise(wo_raw, R, "wo", wo_bf, "late")
        dyq = quantise(dy_raw, N, "dy", dy_bf[:], "dy_codes")
        nc.scalar.copy(mix_n, mix_c.to_broadcast([P, N]))
        nc.scalar.activation(mix_og, mix_c, ACT.Copy, scale=og_c)
        nc.scalar.activation(mix2_og, mix_og, ACT.Copy, scale=mix_c)
        nc.scalar.activation(m2_mix_og, mix_og, ACT.Copy, scale=-2.0)

        v1 = sb.tile([P, N], F32, name="v1")
        nc.vector.tensor_tensor(v1[:], s[:].indirect(idx3[:]), mix_n, MULT)
        th = sb.tile([P, N], F32, name="th")
        nc.scalar.activation(th[:], v1[:], ACT.Tanh, scale=0.5)
        q4 = sb.tile([P, N], F32, name="q4")
        nc.scalar.activation(q4[:], th[:], ACT.Square, scale=0.5)
        sig = sb.tile([P, N], F32, name="sig")
        nc.scalar.activation(sig[:], th[:], ACT.Copy, bias=0.5, scale=0.5)

        c0 = psum.tile([P, N], F32, name="c0", tag="a0")
        product(c0[:], woq, dyq)
        base_sb = sb.tile([P, J], F32, name="base_sb", tag="late", align_bytes=64)
        nc.sync.dma_start(base_sb[:], base)
        cm2 = sb.tile([P, N], F32, name="cm2")
        nc.scalar.activation(cm2[:], c0[:], ACT.Copy, scale=mix2_og)
        cm = sb.tile([P, N], F32, name="cm")
        nc.scalar.activation(cm[:], c0[:], ACT.Copy, scale=m2_mix_og)
        qn = sb.tile([P, N], F32, name="qn")
        nc.scalar.activation(qn[:], q4[:], ACT.Copy, bias=-0.25, scale=1.0)

        nc.vector.scalar_tensor_tensor(xh2[:, :J], ta[:], gain_c, om[:], MULT, MULT)
        xs = sb.tile([P, M], F32, name="xs", tag="sq1", align_bytes=64)
        nc.vector.tensor_copy(xs[:], xh2[:].indirect(idx2[:]))

        a1 = sb.tile([P, N], F32, name="a1")
        nc.vector.scalar_tensor_tensor(a1[:], q4[:], 0.25, v1[:], SUB, MULT)
        b1 = sb.tile([P, N], F32, name="b1")
        nc.vector.tensor_tensor(b1[:], v1[:], th[:], MULT)
        y = sb.tile([P, N], F32, name="y")
        nc.vector.tensor_tensor(y[:], xs[:].indirect(idx3[:]), cm2[:], MULT)
        f1 = sb.tile([P, N], F32, name="f1")
        nc.vector.tensor_tensor(f1[:], sig[:], a1[:], SUB)
        c1 = sb.tile([P, N], F32, name="c1")
        nc.vector.scalar_tensor_tensor(c1[:], b1[:], 2.0, y[:], SUB, MULT)
        nc.vector.tensor_tensor(s1[:].indirect(idx3[:]), f1[:], cm[:], MULT)
        nc.vector.tensor_tensor(xs1[:].indirect(idx3[:]), c1[:], qn[:], MULT)

        blocks = [slice(c * P, (c + 1) * P) for c in range(J // P)]
        turned = [psum.tile([P, P], F32, name="turned%d" % c) for c in range(J // P)]
        for c, cols in enumerate(blocks):
            nc.tensor.matmul(turned[c][:], base_sb[:, cols], ident[:], start=True, stop=False, is_transpose=True)

        z1 = sb.tile([P, WIDE], F32, name="z1")
        nc.vector.tensor_tensor(z1[:].indirect(idx2[:]), s1[:], xs[:], MULT)
        t1 = sb.tile([P, J], F32, name="t1")
        for h in halves:
            nc.gpsimd.tensor_tensor(t1[:, h], z1[:, h], h1[:, h], MULT)
        xs2 = sb.tile([P, WIDE], F32, name="xs2")
        nc.vector.tensor_copy(xs2[:].indirect(idx2[:]), xs1[:])

        turned_sb = sb.tile([P, J], F32, name="turned_sb")
        t1b = psum.tile([P, J], F32, name="t1b", tag="pb_ps")
        for c, cols in enumerate(blocks):
            nc.tensor.matmul(turned[c][:], t1[:, cols], ident[:], start=False, stop=True, is_transpose=True)
        for c, cols in enumerate(blocks):
            nc.scalar.copy(turned_sb[:, cols], turned[c][:])
            nc.tensor.transpose(t1b[:, cols], turned_sb[:, cols], ident[:])

        t2 = sb.tile([P, J], F32, name="t2")
        res = sb.tile([P, J], F32, name="res")
        for h in halves:
            nc.vector.scalar_tensor_tensor(t2[:, h], xs2[:, h], gain_c, om[:, h], MULT, MULT)
        for h in halves:
            nc.vector.tensor_tensor(res[:, h], t2[:, h], t1b[:, h], ADD)
            nc.sync.dma_start(out[:, h], res[:, h])
